import numpy as np
import ml_dtypes


def mxq(x, axis, fmt="e4m3"):
    dtype, down = {"e4m3": (ml_dtypes.float8_e4m3fn, 7), "e5m2": (ml_dtypes.float8_e5m2, 14)}[fmt]
    v = np.moveaxis(np.asarray(x, np.float32).astype(ml_dtypes.bfloat16).astype(np.float64), axis, -1)
    blocks = v.reshape(v.shape[:-1] + (-1, 32))
    amax = np.abs(blocks).max(-1, keepdims=True)
    byte = np.maximum(np.where(amax > 0, np.frexp(amax)[1] - 1 + 127, 0) - down, 1)
    scale = np.exp2(byte - 127.0)
    codes = (blocks / scale).astype(np.float32).astype(dtype).astype(np.float64)
    return np.moveaxis((codes * scale).reshape(v.shape), -1, axis)


WIDE = False


def mx_kscale(k):
    if not WIDE:
        return np.ones(k)
    levels = np.array([30, -30])
    if k % 512:
        return np.exp2(np.random.permutation(np.resize(levels, k // 32))).repeat(32)
    a = np.empty((k // 512, 16))
    for p in range(k // 512):
        a[p, :8] = np.random.permutation(np.resize(levels, 8))
        for g in range(8):
            far = levels[np.abs(levels - a[p, g]) >= 10]
            a[p, g + 8] = far[np.random.randint(len(far))]
    return np.exp2(a.ravel()).repeat(32)


BF16 = ml_dtypes.bfloat16


def bf(x):
    return np.asarray(x, np.float32).astype(BF16)


def f64(x):
    return np.asarray(x).astype(np.float64)


M, K, N = 1024, 2048, 512
BETA = 4.0


def setup_inputs():
    t = mx_kscale(K)
    cosines = np.tanh(0.25 * np.random.standard_normal((M, K)))
    conn = 1.5 * np.abs(np.random.standard_normal((M, K)))
    degree = conn.sum(axis=1)
    gain = 1 + 0.1 * np.random.standard_normal(K)
    coords = 20.0 * np.random.standard_normal((K, N))
    return {"cosines": bf(cosines),
            "conn": bf(conn * t),
            "degree": bf(degree),
            "gain": bf(gain * t),
            "coords": bf(coords / t[:, None])}


def reference(cosines, conn, degree, gain, coords):
    p = np.exp(BETA * f64(cosines))
    z = p.sum(axis=1) + f64(degree)
    e = mxq(f64(coords), 0, "e4m3")
    vel = mxq(p * f64(gain), 1, "e5m2") @ e
    dif = mxq(f64(conn), 1, "e4m3") @ e
    return (vel + dif) / z[:, None]

@@ -1,0 +1,368 @@
+from contextlib import ExitStack
+
+import concourse.mybir as mybir
+from concourse.masks import make_identity
+
+F32 = mybir.dt.float32
+BF16 = mybir.dt.bfloat16
+U32 = mybir.dt.uint32
+U8 = mybir.dt.uint8
+E4M3X4 = mybir.dt.float8_e4m3fn_x4
+E5M2X4 = mybir.dt.float8_e5m2_x4
+ACT = mybir.ActivationFunctionType
+MULT = mybir.AluOpType.mult
+ADD = mybir.AluOpType.add
+
+M, K, N = 1024, 2048, 512
+BETA = 4.0
+P = 128
+TILES = M // P
+PASSES = K // 512
+FLOPS = 2 * 2 * M * K * N
+
+LATE = (0, 1, 2, 3)
+
+
+def tile_velocity_connectivity_smoothing_s2_kernel(tc, cosines, conn, degree, gain, coords, out):
+    nc = tc.nc
+    cos_rows = cosines.rearrange("(p t) k -> p t k", t=TILES)
+    conn_rows = conn.rearrange("(p t) k -> p t k", t=TILES)
+    out_rows = out.rearrange("(p t) c -> p t c", t=TILES)
+    coords_rows = coords.rearrange("(g p j) w -> g p j w", p=P, j=4)
+
+    with ExitStack() as ctx:
+        keep = ctx.enter_context(tc.tile_pool(name="keep", bufs=1))
+        ins = ctx.enter_context(tc.tile_pool(name="ins", bufs=1))
+        work = ctx.enter_context(tc.tile_pool(name="work", bufs=3))
+        banks = ctx.enter_context(tc.psum_pool(name="banks", bufs=6))
+        sums = ctx.enter_context(tc.psum_pool(name="sums", bufs=2))
+
+        cos_sb, conn_sb, raw_sb = {}, {}, {}
+        e_codes, e_scales = {}, {}
+        p_sb, a_sb, a_grp, c_grp = {}, {}, {}, {}
+        a_codes, a_scales, c_codes, c_scales = {}, {}, {}, {}
+        bank, acc, res, ordered = {}, {}, {}, {}
+
+        gain_pt = keep.tile([P, PASSES, 4], BF16, name="gain_pt")
+        gain_f = keep.tile([P, PASSES, 4], F32, name="gain_f")
+        deg = keep.tile([P, TILES], BF16, name="deg")
+        ident = keep.tile([P, P], F32, name="ident")
+        gain_row = keep.tile([P, K], BF16, name="gain_row", align_bytes=64)
+        zsum = keep.tile([P, TILES], F32, name="zsum")
+        ztot = keep.tile([P, TILES], F32, name="ztot")
+        rz = keep.tile([P, TILES], F32, name="rz")
+        dummy = keep.tile([P, 1], F32, name="dummy")
+
+        def load_cos(i):
+            cos_sb[i] = ins.tile([P, K], BF16, name="cos%d" % i)
+            nc.sync.dma_start(out=cos_sb[i][:], in_=cos_rows[:, i, :])
+
+        def load_conn(i):
+            conn_sb[i] = ins.tile([P, K], BF16, name="conn%d" % i)
+            nc.sync.dma_start(out=conn_sb[i][:], in_=conn_rows[:, i, :])
+
+        def load_coords(g):
+            raw_sb[g] = ins.tile([P, 4, N], BF16, name="raw%d" % g)
+            nc.sync.dma_start(out=raw_sb[g][:], in_=coords_rows[g])
+
+        def interleave(g, eng):
+            t = keep.tile([P, N, 4], BF16, name="egrp%d" % g, align_bytes=64)
+            e_codes[g, "in"] = t
+            dst = t[:].rearrange("p (c i) t -> p c t i", i=4)
+            src = raw_sb[g][:].rearrange("p t (c i) -> p c t i", i=4)
+            if eng == "v":
+                nc.vector.tensor_copy(out=dst, in_=src)
+            elif eng == "g":
+                for c in range(2):
+                    w = slice(64 * c, 64 * (c + 1))
+                    nc.gpsimd.tensor_scalar(out=dst[:, w], in0=src[:, w], scalar1=1.0, scalar2=0.0, op0=MULT, op1=ADD)
+            else:
+                nc.scalar.copy(dst, src)
+
+        def q_coords(g):
+            e_codes[g] = keep.tile([P, N], U32, name="ecodes%d" % g, align_bytes=64)
+            e_scales[g] = keep.tile([P, N], U8, name="escales%d" % g, align_bytes=64)
+            nc.vector.quantize_mx(out=e_codes[g][:].bitcast(E4M3X4), scales=e_scales[g][:], in_=e_codes[g, "in"][:].rearrange("p w j -> p (w j)"))
+
+        def load_gain_row():
+            nc.sync.dma_start(out=gain_row[:], in_=gain.partition_broadcast(P))
+
+        def exp(i):
+            p_sb[i] = work.tile([P, K], F32, name="p", align_bytes=64)
+            if i in LATE:
+                src = cos_sb[i][:].rearrange("p (n t) -> p t n", t=4)
+                dst = p_sb[i][:].rearrange("p (t n) -> p t n", t=4)
+            else:
+                src = cos_sb[i][:].rearrange("p (n u e) -> p u n e", u=2, e=2)
+                dst = p_sb[i][:].rearrange("p (u n e) -> p u n e", u=2, e=2)
+            nc.scalar.activation(out=dst, in_=src, func=ACT.Exp, scale=BETA, accum_out=zsum[:, i:i + 1])
+
+        def mul(i, h):
+            if h == 0:
+                a_sb[i] = work.tile([P, 2, K // 4, 2], BF16, name="a", align_bytes=64)
+            n = slice(256 * h, 256 * (h + 1))
+            nc.vector.tensor_tensor(
+                out=a_sb[i][:, :, n, :],
+                in0=p_sb[i][:].rearrange("p (u n e) -> p u n e", u=2, e=2)[:, :, n, :],
+                in1=gain_row[:].rearrange("p (n u e) -> p u n e", u=2, e=2)[:, :, n, :],
+                op=MULT)
+
+        def reorder(i):
+            ordered[i] = work.tile([P, 2, K // 4], F32, name="ordered", align_bytes=64)
+            nc.vector.tensor_copy(out=ordered[i][:], in_=conn_sb[i][:].bitcast(F32).rearrange("p (n u) -> p u n", u=2))
+
+        def tr_conn(i, h):
+            b = banks.tile([P, 2, 2 * P], F32, name="bank")
+            bank["c", i, h] = b
+            words = conn_sb[i][:].bitcast(F32)
+            for g in (2 * h, 2 * h + 1):
+                for u in range(2):
+                    src = ordered[i][:, u, P * g:P * (g + 1)] if i in ordered else words[:, 256 * g + u:256 * (g + 1):2]
+                    nc.tensor.transpose(b[:, u, P * (g % 2):P * (g % 2 + 1)], src, ident[:])
+
+        def tr_a(i, h):
+            b = banks.tile([P, 2, 2 * P], F32, name="bank")
+            bank["a", i, h] = b
+            for g in (2 * h, 2 * h + 1):
+                for u in range(2):
+                    nc.tensor.transpose(b[:, u, P * (g % 2):P * (g % 2 + 1)], a_sb[i][:, u, P * g:P * (g + 1), :].rearrange("p n e -> p (n e)").bitcast(F32), ident[:])
+
+        def tr_late(i, g):
+            b = banks.tile([P, 4, P], F32, name="bank")
+            bank["a", i, g] = b
+            for t in range(4):
+                nc.tensor.transpose(b[:, t, :], p_sb[i][:, 512 * t + P * g:512 * t + P * (g + 1)], ident[:])
+
+        def ev(kind, i, h, eng):
+            grp = c_grp if kind == "c" else a_grp
+            if i not in grp:
+                grp[i] = work.tile([P, 2, 2 * P, 4], BF16, name=kind + "grp", align_bytes=64)
+            dst = grp[i][:, h, :, :].rearrange("p r t -> p (r t)").bitcast(F32).rearrange("p (r u) -> p r u", u=2)
+            src = bank[kind, i, h][:].rearrange("p u r -> p r u")
+            if eng == "v":
+                nc.vector.tensor_copy(out=dst, in_=src)
+            else:
+                nc.scalar.copy(dst, src)
+
+        def ev_late(i, g):
+            if i not in a_grp:
+                a_grp[i] = work.tile([P, 2, 2 * P, 4], BF16, name="agrp", align_bytes=64)
+            dst = a_grp[i][:, g // 2, P * (g % 2):P * (g % 2 + 1), :]
+            nc.vector.tensor_tensor(out=dst, in0=bank["a", i, g][:].rearrange("p t r -> p r t"), in1=gain_f[:, g, :].unsqueeze(1).to_broadcast([P, P, 4]), op=MULT)
+
+        def quant(kind, i):
+            grp, codes, scales, dt = (c_grp, c_codes, c_scales, E4M3X4) if kind == "c" else (a_grp, a_codes, a_scales, E5M2X4)
+            codes[i] = work.tile([P, 512], U32, name=kind + "codes", align_bytes=64)
+            scales[i] = work.tile([P, 512], U8, name=kind + "scales", align_bytes=64)
+            nc.vector.quantize_mx(out=codes[i][:].bitcast(dt), scales=scales[i][:], in_=grp[i][:].rearrange("p h r t -> p (h r t)"))
+
+        def mm(kind, i, gs=None):
+            codes, scales, dt = (c_codes, c_scales, E4M3X4) if kind == "c" else (a_codes, a_scales, E5M2X4)
+            for g in range(PASSES) if gs is None else gs:
+                if kind == "c" and g == 0:
+                    acc[i] = sums.tile([P, N], F32, name="acc")
+                cols = slice(P * g, P * (g + 1))
+                nc.tensor.matmul_mx(
+                    out=acc[i][:], lhsT=codes[i][:, cols].bitcast(dt), lhsT_scale=scales[i][:, cols],
+                    rhs=e_codes[g][:].bitcast(E4M3X4), rhs_scale=e_scales[g][:],
+                    start=(kind == "c" and g == 0), stop=(kind == "a" and g == PASSES - 1))
+
+        def zrec(lo, hi):
+            nc.vector.tensor_tensor(out=ztot[:, lo:hi], in0=zsum[:, lo:hi], in1=deg[:, lo:hi], op=ADD)
+            nc.vector.reciprocal(out=rz[:, lo:hi], in_=ztot[:, lo:hi])
+
+        def ev_out(i, eng):
+            res[i] = work.tile([P, N], F32, name="res")
+            if eng == "v":
+                nc.vector.tensor_scalar(out=res[i][:], in0=acc[i][:], scalar1=rz[:, i:i + 1], scalar2=None, op0=MULT)
+            else:
+                nc.scalar.activation(out=res[i][:], in_=acc[i][:], func=ACT.Copy, scale=rz[:, i:i + 1])
+
+        def store(i):
+            nc.sync.dma_start(out=out_rows[:, i, :], in_=res[i][:])
+
+        nc.scalar.dma_start(out=gain_pt[:], in_=gain.rearrange("(g p t) -> p g t", p=P, t=4))
+        nc.scalar.dma_start(out=deg[:], in_=degree.rearrange("(p t) -> p t", t=TILES))
+        load_cos(0)
+        load_coords(0)
+        load_conn(0)
+        load_coords(1)
+        load_cos(1)
+        load_coords(2)
+        load_conn(1)
+        load_coords(3)
+        load_cos(2)
+        load_conn(2)
+        load_cos(3)
+        load_conn(3)
+        load_gain_row()
+        load_cos(4)
+        load_conn(4)
+        load_cos(5)
+        load_conn(5)
+        load_cos(6)
+        load_conn(6)
+        load_cos(7)
+        load_conn(7)
+        nc.vector.memset(dummy[:], 0.0)
+        make_identity(nc, ident[:])
+        nc.scalar.activation(out=dummy[:], in_=dummy[:], func=ACT.Exp)
+        nc.vector.tensor_copy(out=gain_f[:], in_=gain_pt[:])
+        exp(0)
+        interleave(0, "v")
+        q_coords(0)
+        tr_conn(0, 0)
+        tr_conn(0, 1)
+        ev("c", 0, 0, "s")
+        ev("c", 0, 1, "s")
+        tr_late(0, 0)
+        tr_late(0, 1)
+        tr_late(0, 2)
+        tr_late(0, 3)
+        interleave(1, "v")
+        quant("c", 0)
+        q_coords(1)
+        ev_late(0, 0)
+        ev_late(0, 1)
+        ev_late(0, 2)
+        ev_late(0, 3)
+        exp(1)
+        mm("c", 0, (0, 1))
+        tr_conn(1, 0)
+        tr_conn(1, 1)
+        interleave(2, "s")
+        quant("a", 0)
+        ev("c", 1, 0, "s")
+        ev("c", 1, 1, "s")
+        interleave(3, "v")
+        quant("c", 1)
+        q_coords(2)
+        q_coords(3)
+        tr_late(1, 0)
+        tr_late(1, 1)
+        tr_late(1, 2)
+        tr_late(1, 3)
+        exp(2)
+        mm("a", 0, (0, 1))
+        mm("c", 0, (2, 3))
+        mm("a", 0, (2, 3))
+        zrec(0, 2)
+        ev_late(1, 0)
+        ev_late(1, 1)
+        ev_late(1, 2)
+        ev_late(1, 3)
+        tr_conn(2, 0)
+        tr_conn(2, 1)
+        ev("c", 2, 0, "s")
+        ev("c", 2, 1, "s")
+        quant("a", 1)
+        quant("c", 2)
+        exp(3)
+        tr_late(2, 0)
+        tr_late(2, 1)
+        tr_late(2, 2)
+        tr_late(2, 3)
+        ev_out(0, "s")
+        store(0)
+        ev_late(2, 0)
+        ev_late(2, 1)
+        ev_late(2, 2)
+        ev_late(2, 3)
+        tr_conn(3, 0)
+        tr_conn(3, 1)
+        mm("c", 1)
+        mm("a", 1)
+        ev("c", 3, 0, "s")
+        ev("c", 3, 1, "s")
+        quant("a", 2)
+        quant("c", 3)
+        exp(4)
+        tr_late(3, 0)
+        tr_late(3, 1)
+        tr_late(3, 2)
+        tr_late(3, 3)
+        ev_out(1, "s")
+        store(1)
+        zrec(2, 4)
+        ev_late(3, 0)
+        ev_late(3, 1)
+        ev_late(3, 2)
+        ev_late(3, 3)
+        tr_conn(4, 0)
+        tr_conn(4, 1)
+        mm("c", 2)
+        mm("a", 2)
+        ev("c", 4, 0, "s")
+        ev("c", 4, 1, "s")
+        quant("a", 3)
+        mul(4, 0)
+        quant("c", 4)
+        mul(4, 1)
+        exp(5)
+        tr_a(4, 0)
+        tr_a(4, 1)
+        ev_out(2, "s")
+        store(2)
+        tr_conn(5, 0)
+        tr_conn(5, 1)
+        mm("c", 3)
+        mm("a", 3)
+        ev("c", 5, 0, "s")
+        ev("c", 5, 1, "s")
+        ev("a", 4, 0, "s")
+        ev("a", 4, 1, "v")
+        quant("a", 4)
+        mul(5, 0)
+        quant("c", 5)
+        mul(5, 1)
+        exp(6)
+        tr_a(5, 0)
+        tr_a(5, 1)
+        ev_out(3, "s")
+        store(3)
+        zrec(4, 6)
+        tr_conn(6, 0)
+        tr_conn(6, 1)
+        mm("c", 4)
+        mm("a", 4)
+        ev("c", 6, 0, "s")
+        ev("c", 6, 1, "s")
+        ev("a", 5, 0, "s")
+        ev("a", 5, 1, "v")
+        quant("a", 5)
+        mul(6, 0)
+        quant("c", 6)
+        mul(6, 1)
+        exp(7)
+        tr_a(6, 0)
+        tr_a(6, 1)
+        ev_out(4, "s")
+        store(4)
+        tr_conn(7, 0)
+        tr_conn(7, 1)
+        mm("c", 5)
+        mm("a", 5)
+        ev("c", 7, 0, "s")
+        ev("c", 7, 1, "s")
+        ev("a", 6, 0, "s")
+        ev("a", 6, 1, "v")
+        quant("a", 6)
+        mul(7, 0)
+        quant("c", 7)
+        mul(7, 1)
+        tr_a(7, 0)
+        tr_a(7, 1)
+        ev_out(5, "s")
+        store(5)
+        zrec(6, 8)
+        mm("c", 6)
+        mm("a", 6)
+        ev("a", 7, 0, "s")
+        ev("a", 7, 1, "v")
+        quant("a", 7)
+        ev_out(6, "s")
+        store(6)
+        mm("c", 7)
+        mm("a", 7)
+        ev_out(7, "s")
+        store(7)

@@ -20,7 +20,7 @@ TILES = M // P
 PASSES = K // 512
 FLOPS = 2 * 2 * M * K * N
 
-LATE = (0, 1, 2, 3)
+LATE = tuple(range(3))
 
 
 def tile_velocity_connectivity_smoothing_s2_kernel(tc, cosines, conn, degree, gain, coords, out):
@@ -36,6 +36,7 @@ def tile_velocity_connectivity_smoothing_s2_kernel(tc, cosines, conn, degree, ga
         work = ctx.enter_context(tc.tile_pool(name="work", bufs=3))
         banks = ctx.enter_context(tc.psum_pool(name="banks", bufs=6))
         sums = ctx.enter_context(tc.psum_pool(name="sums", bufs=2))
+        ctx.enter_context(tc.manual_schedule(engines={mybir.EngineType.PE, mybir.EngineType.SP}))
 
         cos_sb, conn_sb, raw_sb = {}, {}, {}
         e_codes, e_scales = {}, {}
@@ -51,11 +52,14 @@ def tile_velocity_connectivity_smoothing_s2_kernel(tc, cosines, conn, degree, ga
         zsum = keep.tile([P, TILES], F32, name="zsum")
         ztot = keep.tile([P, TILES], F32, name="ztot")
         rz = keep.tile([P, TILES], F32, name="rz")
+        zhalf = keep.tile([P, 2], F32, name="zhalf")
         dummy = keep.tile([P, 1], F32, name="dummy")
 
-        def load_cos(i):
-            cos_sb[i] = ins.tile([P, K], BF16, name="cos%d" % i)
-            nc.sync.dma_start(out=cos_sb[i][:], in_=cos_rows[:, i, :])
+        def load_cos(i, h=None):
+            if i not in cos_sb:
+                cos_sb[i] = ins.tile([P, K], BF16, name="cos%d" % i)
+            c = slice(0, K) if h is None else slice(K // 2 * h, K // 2 * (h + 1))
+            nc.sync.dma_start(out=cos_sb[i][:, c], in_=cos_rows[:, i, c])
 
         def load_conn(i):
             conn_sb[i] = ins.tile([P, K], BF16, name="conn%d" % i)
@@ -84,8 +88,19 @@ def tile_velocity_connectivity_smoothing_s2_kernel(tc, cosines, conn, degree, ga
             e_scales[g] = keep.tile([P, N], U8, name="escales%d" % g, align_bytes=64)
             nc.vector.quantize_mx(out=e_codes[g][:].bitcast(E4M3X4), scales=e_scales[g][:], in_=e_codes[g, "in"][:].rearrange("p w j -> p (w j)"))
 
-        def load_gain_row():
-            nc.sync.dma_start(out=gain_row[:], in_=gain.partition_broadcast(P))
+        def load_gain_row(g):
+            c = slice(512 * g, 512 * (g + 1))
+            nc.sync.dma_start(out=gain_row[:, c], in_=gain[c].partition_broadcast(P))
+
+        def exp_half(i, h):
+            if h == 0:
+                p_sb[i] = work.tile([P, K], F32, name="p", align_bytes=64)
+            n = slice(256 * h, 256 * (h + 1))
+            src = cos_sb[i][:].rearrange("p (n t) -> p t n", t=4)[:, :, n]
+            dst = p_sb[i][:].rearrange("p (t n) -> p t n", t=4)[:, :, n]
+            nc.scalar.activation(out=dst, in_=src, func=ACT.Exp, scale=BETA, accum_out=zhalf[:, h:h + 1])
+            if h == 1:
+                nc.vector.tensor_tensor(out=zsum[:, i:i + 1], in0=zhalf[:, 0:1], in1=zhalf[:, 1:2], op=ADD)
 
         def exp(i):
             p_sb[i] = work.tile([P, K], F32, name="p", align_bytes=64)
@@ -97,10 +112,10 @@ def tile_velocity_connectivity_smoothing_s2_kernel(tc, cosines, conn, degree, ga
                 dst = p_sb[i][:].rearrange("p (u n e) -> p u n e", u=2, e=2)
             nc.scalar.activation(out=dst, in_=src, func=ACT.Exp, scale=BETA, accum_out=zsum[:, i:i + 1])
 
-        def mul(i, h):
-            if h == 0:
+        def mul(i, h=None):
+            if not h:
                 a_sb[i] = work.tile([P, 2, K // 4, 2], BF16, name="a", align_bytes=64)
-            n = slice(256 * h, 256 * (h + 1))
+            n = slice(0, 512) if h is None else slice(256 * h, 256 * (h + 1))
             nc.vector.tensor_tensor(
                 out=a_sb[i][:, :, n, :],
                 in0=p_sb[i][:].rearrange("p (u n e) -> p u n e", u=2, e=2)[:, :, n, :],
@@ -150,11 +165,13 @@ def tile_velocity_connectivity_smoothing_s2_kernel(tc, cosines, conn, degree, ga
             dst = a_grp[i][:, g // 2, P * (g % 2):P * (g % 2 + 1), :]
             nc.vector.tensor_tensor(out=dst, in0=bank["a", i, g][:].rearrange("p t r -> p r t"), in1=gain_f[:, g, :].unsqueeze(1).to_broadcast([P, P, 4]), op=MULT)
 
-        def quant(kind, i):
+        def quant(kind, i, h=None):
             grp, codes, scales, dt = (c_grp, c_codes, c_scales, E4M3X4) if kind == "c" else (a_grp, a_codes, a_scales, E5M2X4)
-            codes[i] = work.tile([P, 512], U32, name=kind + "codes", align_bytes=64)
-            scales[i] = work.tile([P, 512], U8, name=kind + "scales", align_bytes=64)
-            nc.vector.quantize_mx(out=codes[i][:].bitcast(dt), scales=scales[i][:], in_=grp[i][:].rearrange("p h r t -> p (h r t)"))
+            if not h:
+                codes[i] = work.tile([P, 512], U32, name=kind + "codes", align_bytes=64)
+                scales[i] = work.tile([P, 512], U8, name=kind + "scales", align_bytes=64)
+            w = slice(0, 512) if h is None else slice(256 * h, 256 * (h + 1))
+            nc.vector.quantize_mx(out=codes[i][:, w].bitcast(dt), scales=scales[i][:, w], in_=grp[i][:].rearrange("p h r t -> p (h r t)")[:, 4 * w.start:4 * w.stop])
 
         def mm(kind, i, gs=None):
             codes, scales, dt = (c_codes, c_scales, E4M3X4) if kind == "c" else (a_codes, a_scales, E5M2X4)
@@ -171,31 +188,36 @@ def tile_velocity_connectivity_smoothing_s2_kernel(tc, cosines, conn, degree, ga
             nc.vector.tensor_tensor(out=ztot[:, lo:hi], in0=zsum[:, lo:hi], in1=deg[:, lo:hi], op=ADD)
             nc.vector.reciprocal(out=rz[:, lo:hi], in_=ztot[:, lo:hi])
 
-        def ev_out(i, eng):
-            res[i] = work.tile([P, N], F32, name="res")
+        def ev_out(i, eng, c=slice(0, N)):
+            if c.start == 0:
+                res[i] = work.tile([P, N], F32, name="res")
             if eng == "v":
-                nc.vector.tensor_scalar(out=res[i][:], in0=acc[i][:], scalar1=rz[:, i:i + 1], scalar2=None, op0=MULT)
+                nc.vector.tensor_scalar(out=res[i][:, c], in0=acc[i][:, c], scalar1=rz[:, i:i + 1], scalar2=None, op0=MULT)
             else:
-                nc.scalar.activation(out=res[i][:], in_=acc[i][:], func=ACT.Copy, scale=rz[:, i:i + 1])
+                nc.scalar.activation(out=res[i][:, c], in_=acc[i][:, c], func=ACT.Copy, scale=rz[:, i:i + 1])
 
-        def store(i):
-            nc.sync.dma_start(out=out_rows[:, i, :], in_=res[i][:])
+        def store(i, c=slice(0, N)):
+            nc.sync.dma_start(out=out_rows[:, i, c], in_=res[i][:, c])
 
-        nc.scalar.dma_start(out=gain_pt[:], in_=gain.rearrange("(g p t) -> p g t", p=P, t=4))
-        nc.scalar.dma_start(out=deg[:], in_=degree.rearrange("(p t) -> p t", t=TILES))
-        load_cos(0)
+        load_cos(0, 0)
         load_coords(0)
+        load_cos(0, 1)
         load_conn(0)
+        nc.sync.dma_start(out=gain_pt[:], in_=gain.rearrange("(g p t) -> p g t", p=P, t=4))
+        nc.sync.dma_start(out=deg[:], in_=degree.rearrange("(p t) -> p t", t=TILES))
         load_coords(1)
         load_cos(1)
         load_coords(2)
         load_conn(1)
         load_coords(3)
         load_cos(2)
+        load_gain_row(0)
         load_conn(2)
+        load_gain_row(1)
         load_cos(3)
+        load_gain_row(2)
         load_conn(3)
-        load_gain_row()
+        load_gain_row(3)
         load_cos(4)
         load_conn(4)
         load_cos(5)
@@ -208,161 +230,167 @@ def tile_velocity_connectivity_smoothing_s2_kernel(tc, cosines, conn, degree, ga
         make_identity(nc, ident[:])
         nc.scalar.activation(out=dummy[:], in_=dummy[:], func=ACT.Exp)
         nc.vector.tensor_copy(out=gain_f[:], in_=gain_pt[:])
-        exp(0)
+        exp_half(0, 0)
+        exp_half(0, 1)
         interleave(0, "v")
         q_coords(0)
-        tr_conn(0, 0)
-        tr_conn(0, 1)
-        ev("c", 0, 0, "s")
-        ev("c", 0, 1, "s")
         tr_late(0, 0)
-        tr_late(0, 1)
-        tr_late(0, 2)
-        tr_late(0, 3)
-        interleave(1, "v")
-        quant("c", 0)
-        q_coords(1)
         ev_late(0, 0)
+        tr_late(0, 1)
         ev_late(0, 1)
+        tr_conn(0, 0)
+        ev("c", 0, 0, "s")
+        tr_conn(0, 1)
+        ev("c", 0, 1, "s")
+        quant("c", 0)
+        tr_late(0, 2)
         ev_late(0, 2)
+        tr_late(0, 3)
         ev_late(0, 3)
-        exp(1)
-        mm("c", 0, (0, 1))
-        tr_conn(1, 0)
-        tr_conn(1, 1)
-        interleave(2, "s")
         quant("a", 0)
-        ev("c", 1, 0, "s")
-        ev("c", 1, 1, "s")
-        interleave(3, "v")
-        quant("c", 1)
-        q_coords(2)
-        q_coords(3)
-        tr_late(1, 0)
-        tr_late(1, 1)
-        tr_late(1, 2)
-        tr_late(1, 3)
-        exp(2)
-        mm("a", 0, (0, 1))
-        mm("c", 0, (2, 3))
-        mm("a", 0, (2, 3))
+        exp(1)
         zrec(0, 2)
+        interleave(1, "v")
+        q_coords(1)
+        tr_conn(1, 0)
+        ev("c", 1, 0, "s")
+        tr_conn(1, 1)
+        ev("c", 1, 1, "s")
+        quant("c", 1)
+        tr_late(1, 0)
         ev_late(1, 0)
+        tr_late(1, 1)
         ev_late(1, 1)
+        tr_late(1, 2)
         ev_late(1, 2)
+        tr_late(1, 3)
         ev_late(1, 3)
-        tr_conn(2, 0)
-        tr_conn(2, 1)
-        ev("c", 2, 0, "s")
-        ev("c", 2, 1, "s")
         quant("a", 1)
+        interleave(2, "s")
+        q_coords(2)
+        mm("c", 0, (0,))
+        mm("a", 0, (0,))
+        mm("c", 0, (1,))
+        mm("a", 0, (1,))
+        exp(2)
+        tr_conn(2, 0)
+        ev("c", 2, 0, "s")
+        tr_conn(2, 1)
+        ev("c", 2, 1, "s")
         quant("c", 2)
-        exp(3)
-        tr_late(2, 0)
-        tr_late(2, 1)
-        tr_late(2, 2)
-        tr_late(2, 3)
+        interleave(3, "v")
+        q_coords(3)
+        mm("c", 0, (2,))
+        mm("a", 0, (2,))
+        mm("c", 0, (3,))
+        mm("a", 0, (3,))
         ev_out(0, "s")
         store(0)
+        exp(3)
+        zrec(2, 4)
+        tr_late(2, 0)
         ev_late(2, 0)
+        tr_late(2, 1)
         ev_late(2, 1)
+        tr_late(2, 2)
         ev_late(2, 2)
+        tr_late(2, 3)
         ev_late(2, 3)
+        quant("a", 2)
         tr_conn(3, 0)
+        ev("c", 3, 0, "s")
         tr_conn(3, 1)
+        ev("c", 3, 1, "s")
+        quant("c", 3)
+        mul(3, 0)
+        mul(3, 1)
         mm("c", 1)
         mm("a", 1)
-        ev("c", 3, 0, "s")
-        ev("c", 3, 1, "s")
-        quant("a", 2)
-        quant("c", 3)
-        exp(4)
-        tr_late(3, 0)
-        tr_late(3, 1)
-        tr_late(3, 2)
-        tr_late(3, 3)
         ev_out(1, "s")
         store(1)
-        zrec(2, 4)
-        ev_late(3, 0)
-        ev_late(3, 1)
-        ev_late(3, 2)
-        ev_late(3, 3)
+        exp(4)
+        tr_a(3, 0)
+        ev("a", 3, 0, "s")
+        tr_a(3, 1)
+        ev("a", 3, 1, "v")
+        quant("a", 3)
         tr_conn(4, 0)
+        ev("c", 4, 0, "s")
         tr_conn(4, 1)
+        ev("c", 4, 1, "s")
+        quant("c", 4)
+        mul(4, 0)
+        mul(4, 1)
         mm("c", 2)
         mm("a", 2)
-        ev("c", 4, 0, "s")
-        ev("c", 4, 1, "s")
-        quant("a", 3)
-        mul(4, 0)
-        quant("c", 4)
-        mul(4, 1)
-        exp(5)
-        tr_a(4, 0)
-        tr_a(4, 1)
         ev_out(2, "s")
         store(2)
-        tr_conn(5, 0)
-        tr_conn(5, 1)
-        mm("c", 3)
-        mm("a", 3)
-        ev("c", 5, 0, "s")
-        ev("c", 5, 1, "s")
+        exp(5)
+        zrec(4, 6)
+        tr_a(4, 0)
         ev("a", 4, 0, "s")
+        tr_a(4, 1)
         ev("a", 4, 1, "v")
         quant("a", 4)
-        mul(5, 0)
+        tr_conn(5, 0)
+        ev("c", 5, 0, "s")
+        tr_conn(5, 1)
+        ev("c", 5, 1, "s")
         quant("c", 5)
+        mul(5, 0)
         mul(5, 1)
-        exp(6)
-        tr_a(5, 0)
-        tr_a(5, 1)
+        mm("c", 3)
+        mm("a", 3)
         ev_out(3, "s")
         store(3)
-        zrec(4, 6)
-        tr_conn(6, 0)
-        tr_conn(6, 1)
-        mm("c", 4)
-        mm("a", 4)
-        ev("c", 6, 0, "s")
-        ev("c", 6, 1, "s")
+        exp(6)
+        tr_a(5, 0)
         ev("a", 5, 0, "s")
+        tr_a(5, 1)
         ev("a", 5, 1, "v")
         quant("a", 5)
-        mul(6, 0)
+        tr_conn(6, 0)
+        ev("c", 6, 0, "s")
+        tr_conn(6, 1)
+        ev("c", 6, 1, "s")
         quant("c", 6)
+        mul(6, 0)
         mul(6, 1)
-        exp(7)
-        tr_a(6, 0)
-        tr_a(6, 1)
+        mm("c", 4)
+        mm("a", 4)
         ev_out(4, "s")
         store(4)
-        tr_conn(7, 0)
-        tr_conn(7, 1)
-        mm("c", 5)
-        mm("a", 5)
-        ev("c", 7, 0, "s")
-        ev("c", 7, 1, "s")
+        exp(7)
+        zrec(6, 8)
+        tr_a(6, 0)
         ev("a", 6, 0, "s")
+        tr_a(6, 1)
         ev("a", 6, 1, "v")
         quant("a", 6)
-        mul(7, 0)
+        tr_conn(7, 0)
+        ev("c", 7, 0, "s")
+        tr_conn(7, 1)
+        ev("c", 7, 1, "s")
         quant("c", 7)
+        mul(7, 0)
         mul(7, 1)
-        tr_a(7, 0)
-        tr_a(7, 1)
+        mm("c", 5)
+        mm("a", 5)
         ev_out(5, "s")
         store(5)
-        zrec(6, 8)
+        tr_a(7, 0)
+        ev("a", 7, 0, "s")
+        tr_a(7, 1)
+        ev("a", 7, 1, "v")
+        quant("a", 7, 0)
+        quant("a", 7, 1)
         mm("c", 6)
         mm("a", 6)
-        ev("a", 7, 0, "s")
-        ev("a", 7, 1, "v")
-        quant("a", 7)
         ev_out(6, "s")
         store(6)
         mm("c", 7)
         mm("a", 7)
-        ev_out(7, "s")
-        store(7)
+        ev_out(7, "s", slice(0, 256))
+        store(7, slice(0, 256))
+        ev_out(7, "v", slice(256, 512))
+        store(7, slice(256, 512))

@@ -20,7 +20,8 @@ TILES = M // P
 PASSES = K // 512
 FLOPS = 2 * 2 * M * K * N
 
-LATE = tuple(range(3))
+LATE = tuple(range(2))
+HALF = True
 
 
 def tile_velocity_connectivity_smoothing_s2_kernel(tc, cosines, conn, degree, gain, coords, out):
@@ -36,7 +37,7 @@ def tile_velocity_connectivity_smoothing_s2_kernel(tc, cosines, conn, degree, ga
         work = ctx.enter_context(tc.tile_pool(name="work", bufs=3))
         banks = ctx.enter_context(tc.psum_pool(name="banks", bufs=6))
         sums = ctx.enter_context(tc.psum_pool(name="sums", bufs=2))
-        ctx.enter_context(tc.manual_schedule(engines={mybir.EngineType.PE, mybir.EngineType.SP}))
+        ctx.enter_context(tc.manual_schedule())
 
         cos_sb, conn_sb, raw_sb = {}, {}, {}
         e_codes, e_scales = {}, {}
@@ -53,6 +54,7 @@ def tile_velocity_connectivity_smoothing_s2_kernel(tc, cosines, conn, degree, ga
         ztot = keep.tile([P, TILES], F32, name="ztot")
         rz = keep.tile([P, TILES], F32, name="rz")
         zhalf = keep.tile([P, 2], F32, name="zhalf")
+        zeros = keep.tile([P, N], BF16, name="zeros")
         dummy = keep.tile([P, 1], F32, name="dummy")
 
         def load_cos(i, h=None):
@@ -61,9 +63,19 @@ def tile_velocity_connectivity_smoothing_s2_kernel(tc, cosines, conn, degree, ga
             c = slice(0, K) if h is None else slice(K // 2 * h, K // 2 * (h + 1))
             nc.sync.dma_start(out=cos_sb[i][:, c], in_=cos_rows[:, i, c])
 
-        def load_conn(i):
-            conn_sb[i] = ins.tile([P, K], BF16, name="conn%d" % i)
-            nc.sync.dma_start(out=conn_sb[i][:], in_=conn_rows[:, i, :])
+        def load_conn(i, h=None):
+            if i not in conn_sb:
+                conn_sb[i] = ins.tile([P, K], BF16, name="conn%d" % i)
+            c = slice(0, K) if h is None else slice(K // 2 * h, K // 2 * (h + 1))
+            nc.sync.dma_start(out=conn_sb[i][:, c], in_=conn_rows[:, i, c])
+
+        def load_small():
+            nc.sync.dma_start(out=gain_pt[:], in_=gain.rearrange("(g p t) -> p g t", p=P, t=4))
+            nc.sync.dma_start(out=deg[:], in_=degree.rearrange("(p t) -> p t", t=TILES))
+
+        def dummies(n):
+            for k in range(n):
+                nc.tensor.matmul(acc["warm"][:], lhsT=zeros[:, 0:P], rhs=zeros[:], start=True, stop=True)
 
         def load_coords(g):
             raw_sb[g] = ins.tile([P, 4, N], BF16, name="raw%d" % g)
@@ -99,8 +111,6 @@ def tile_velocity_connectivity_smoothing_s2_kernel(tc, cosines, conn, degree, ga
             src = cos_sb[i][:].rearrange("p (n t) -> p t n", t=4)[:, :, n]
             dst = p_sb[i][:].rearrange("p (t n) -> p t n", t=4)[:, :, n]
             nc.scalar.activation(out=dst, in_=src, func=ACT.Exp, scale=BETA, accum_out=zhalf[:, h:h + 1])
-            if h == 1:
-                nc.vector.tensor_tensor(out=zsum[:, i:i + 1], in0=zhalf[:, 0:1], in1=zhalf[:, 1:2], op=ADD)
 
         def exp(i):
             p_sb[i] = work.tile([P, K], F32, name="p", align_bytes=64)
@@ -185,6 +195,8 @@ def tile_velocity_connectivity_smoothing_s2_kernel(tc, cosines, conn, degree, ga
                     start=(kind == "c" and g == 0), stop=(kind == "a" and g == PASSES - 1))
 
         def zrec(lo, hi):
+            if HALF and lo == 0:
+                nc.vector.tensor_tensor(out=zsum[:, 0:1], in0=zhalf[:, 0:1], in1=zhalf[:, 1:2], op=ADD)
             nc.vector.tensor_tensor(out=ztot[:, lo:hi], in0=zsum[:, lo:hi], in1=deg[:, lo:hi], op=ADD)
             nc.vector.reciprocal(out=rz[:, lo:hi], in_=ztot[:, lo:hi])
 
@@ -199,25 +211,29 @@ def tile_velocity_connectivity_smoothing_s2_kernel(tc, cosines, conn, degree, ga
         def store(i, c=slice(0, N)):
             nc.sync.dma_start(out=out_rows[:, i, c], in_=res[i][:, c])
 
+        nc.vector.memset(zeros[:], 0.0)
+        nc.vector.memset(dummy[:], 0.0)
+        make_identity(nc, ident[:])
+        nc.scalar.activation(out=dummy[:], in_=dummy[:], func=ACT.Exp)
         load_cos(0, 0)
+        load_conn(0, 0)
         load_coords(0)
+        load_small()
         load_cos(0, 1)
-        load_conn(0)
-        nc.sync.dma_start(out=gain_pt[:], in_=gain.rearrange("(g p t) -> p g t", p=P, t=4))
-        nc.sync.dma_start(out=deg[:], in_=degree.rearrange("(p t) -> p t", t=TILES))
-        load_coords(1)
+        load_conn(0, 1)
         load_cos(1)
-        load_coords(2)
+        load_coords(1)
         load_conn(1)
+        load_coords(2)
         load_coords(3)
         load_cos(2)
-        load_gain_row(0)
         load_conn(2)
+        load_gain_row(0)
         load_gain_row(1)
-        load_cos(3)
         load_gain_row(2)
-        load_conn(3)
         load_gain_row(3)
+        load_cos(3)
+        load_conn(3)
         load_cos(4)
         load_conn(4)
         load_cos(5)
@@ -226,170 +242,177 @@ def tile_velocity_connectivity_smoothing_s2_kernel(tc, cosines, conn, degree, ga
         load_conn(6)
         load_cos(7)
         load_conn(7)
-        nc.vector.memset(dummy[:], 0.0)
-        make_identity(nc, ident[:])
-        nc.scalar.activation(out=dummy[:], in_=dummy[:], func=ACT.Exp)
-        nc.vector.tensor_copy(out=gain_f[:], in_=gain_pt[:])
+        acc["warm"] = sums.tile([P, N], F32, name="acc")
+        dummies(7)
         exp_half(0, 0)
         exp_half(0, 1)
         interleave(0, "v")
-        q_coords(0)
+        nc.vector.tensor_copy(out=gain_f[:], in_=gain_pt[:])
         tr_late(0, 0)
-        ev_late(0, 0)
         tr_late(0, 1)
-        ev_late(0, 1)
+        dummies(2)
         tr_conn(0, 0)
-        ev("c", 0, 0, "s")
         tr_conn(0, 1)
-        ev("c", 0, 1, "s")
-        quant("c", 0)
+        dummies(2)
         tr_late(0, 2)
-        ev_late(0, 2)
         tr_late(0, 3)
-        ev_late(0, 3)
-        quant("a", 0)
+        ev_late(0, 0)
+        ev_late(0, 1)
+        q_coords(0)
+        ev("c", 0, 0, "s")
+        ev("c", 0, 1, "s")
         exp(1)
-        zrec(0, 2)
         interleave(1, "v")
-        q_coords(1)
+        ev_late(0, 2)
+        ev_late(0, 3)
+        quant("c", 0)
+        dummies(2)
         tr_conn(1, 0)
-        ev("c", 1, 0, "s")
         tr_conn(1, 1)
-        ev("c", 1, 1, "s")
-        quant("c", 1)
+        dummies(2)
         tr_late(1, 0)
-        ev_late(1, 0)
         tr_late(1, 1)
-        ev_late(1, 1)
         tr_late(1, 2)
-        ev_late(1, 2)
         tr_late(1, 3)
-        ev_late(1, 3)
-        quant("a", 1)
-        interleave(2, "s")
-        q_coords(2)
+        ev("c", 1, 0, "s")
+        ev("c", 1, 1, "v")
+        quant("a", 0)
         mm("c", 0, (0,))
         mm("a", 0, (0,))
+        ev_late(1, 0)
+        ev_late(1, 1)
+        ev_late(1, 2)
+        ev_late(1, 3)
+        tr_conn(2, 0)
+        tr_conn(2, 1)
+        quant("c", 1)
+        quant("a", 1)
+        q_coords(1)
+        interleave(2, "s")
+        mm("c", 1, (0,))
+        mm("a", 1, (0,))
         mm("c", 0, (1,))
         mm("a", 0, (1,))
+        mm("c", 1, (1,))
+        mm("a", 1, (1,))
         exp(2)
-        tr_conn(2, 0)
-        ev("c", 2, 0, "s")
-        tr_conn(2, 1)
-        ev("c", 2, 1, "s")
-        quant("c", 2)
-        interleave(3, "v")
+        interleave(3, "s")
+        exp(3)
+        mul(2, 0)
+        mul(2, 1)
+        tr_a(2, 0)
+        tr_a(2, 1)
+        q_coords(2)
         q_coords(3)
         mm("c", 0, (2,))
         mm("a", 0, (2,))
+        mm("c", 1, (2,))
+        mm("a", 1, (2,))
         mm("c", 0, (3,))
         mm("a", 0, (3,))
+        mm("c", 1, (3,))
+        mm("a", 1, (3,))
+        ev("c", 2, 0, "s")
+        ev("c", 2, 1, "v")
+        zrec(0, 2)
+        ev("a", 2, 0, "s")
         ev_out(0, "s")
         store(0)
-        exp(3)
-        zrec(2, 4)
-        tr_late(2, 0)
-        ev_late(2, 0)
-        tr_late(2, 1)
-        ev_late(2, 1)
-        tr_late(2, 2)
-        ev_late(2, 2)
-        tr_late(2, 3)
-        ev_late(2, 3)
-        quant("a", 2)
-        tr_conn(3, 0)
-        ev("c", 3, 0, "s")
-        tr_conn(3, 1)
-        ev("c", 3, 1, "s")
-        quant("c", 3)
+        ev("a", 2, 1, "s")
+        exp(4)
+        quant("c", 2)
         mul(3, 0)
         mul(3, 1)
-        mm("c", 1)
-        mm("a", 1)
-        ev_out(1, "s")
+        quant("a", 2)
+        ev_out(1, "v")
         store(1)
-        exp(4)
+        tr_conn(3, 0)
+        tr_conn(3, 1)
+        mm("c", 2, (0, 1, 2, 3,))
         tr_a(3, 0)
-        ev("a", 3, 0, "s")
         tr_a(3, 1)
-        ev("a", 3, 1, "v")
-        quant("a", 3)
-        tr_conn(4, 0)
-        ev("c", 4, 0, "s")
-        tr_conn(4, 1)
-        ev("c", 4, 1, "s")
-        quant("c", 4)
+        mm("a", 2, (0, 1, 2, 3,))
+        ev("c", 3, 0, "s")
+        ev("c", 3, 1, "v")
+        ev("a", 3, 0, "s")
+        ev("a", 3, 1, "s")
+        zrec(2, 4)
+        exp(5)
+        quant("c", 3)
         mul(4, 0)
         mul(4, 1)
-        mm("c", 2)
-        mm("a", 2)
+        quant("a", 3)
+        tr_conn(4, 0)
+        tr_conn(4, 1)
+        mm("c", 3, (0, 1, 2, 3,))
+        tr_a(4, 0)
+        tr_a(4, 1)
+        mm("a", 3, (0, 1, 2, 3,))
+        ev("c", 4, 0, "s")
+        ev("c", 4, 1, "v")
+        ev("a", 4, 0, "s")
         ev_out(2, "s")
         store(2)
-        exp(5)
-        zrec(4, 6)
-        tr_a(4, 0)
-        ev("a", 4, 0, "s")
-        tr_a(4, 1)
-        ev("a", 4, 1, "v")
-        quant("a", 4)
-        tr_conn(5, 0)
-        ev("c", 5, 0, "s")
-        tr_conn(5, 1)
-        ev("c", 5, 1, "s")
-        quant("c", 5)
+        ev("a", 4, 1, "s")
+        exp(6)
+        quant("c", 4)
         mul(5, 0)
         mul(5, 1)
-        mm("c", 3)
-        mm("a", 3)
-        ev_out(3, "s")
-        store(3)
-        exp(6)
+        quant("a", 4)
+        tr_conn(5, 0)
+        tr_conn(5, 1)
+        mm("c", 4, (0, 1, 2, 3,))
         tr_a(5, 0)
-        ev("a", 5, 0, "s")
         tr_a(5, 1)
-        ev("a", 5, 1, "v")
-        quant("a", 5)
-        tr_conn(6, 0)
-        ev("c", 6, 0, "s")
-        tr_conn(6, 1)
-        ev("c", 6, 1, "s")
-        quant("c", 6)
+        mm("a", 4, (0, 1, 2, 3,))
+        ev("c", 5, 0, "s")
+        ev("c", 5, 1, "v")
+        ev("a", 5, 0, "s")
+        ev_out(3, "v")
+        store(3)
+        ev("a", 5, 1, "s")
+        zrec(4, 6)
+        exp(7)
+        quant("c", 5)
         mul(6, 0)
         mul(6, 1)
-        mm("c", 4)
-        mm("a", 4)
+        quant("a", 5)
+        tr_conn(6, 0)
+        tr_conn(6, 1)
+        mm("c", 5, (0, 1, 2, 3,))
+        tr_a(6, 0)
+        tr_a(6, 1)
+        mm("a", 5, (0, 1, 2, 3,))
+        ev("c", 6, 0, "s")
+        ev("c", 6, 1, "v")
+        ev("a", 6, 0, "s")
         ev_out(4, "s")
         store(4)
-        exp(7)
-        zrec(6, 8)
-        tr_a(6, 0)
-        ev("a", 6, 0, "s")
-        tr_a(6, 1)
-        ev("a", 6, 1, "v")
-        quant("a", 6)
-        tr_conn(7, 0)
-        ev("c", 7, 0, "s")
-        tr_conn(7, 1)
-        ev("c", 7, 1, "s")
-        quant("c", 7)
+        ev("a", 6, 1, "s")
+        quant("c", 6)
         mul(7, 0)
         mul(7, 1)
-        mm("c", 5)
-        mm("a", 5)
-        ev_out(5, "s")
-        store(5)
+        quant("a", 6)
+        tr_conn(7, 0)
+        tr_conn(7, 1)
+        mm("c", 6, (0, 1, 2, 3,))
         tr_a(7, 0)
-        ev("a", 7, 0, "s")
         tr_a(7, 1)
-        ev("a", 7, 1, "v")
+        mm("a", 6, (0, 1, 2, 3,))
+        ev("c", 7, 0, "s")
+        ev("c", 7, 1, "v")
+        ev("a", 7, 0, "s")
+        ev_out(5, "v")
+        store(5)
+        ev("a", 7, 1, "s")
+        zrec(6, 8)
+        quant("c", 7)
         quant("a", 7, 0)
         quant("a", 7, 1)
-        mm("c", 6)
-        mm("a", 6)
+        mm("c", 7, (0, 1, 2, 3,))
+        mm("a", 7, (0, 1, 2, 3,))
         ev_out(6, "s")
         store(6)
-        mm("c", 7)
-        mm("a", 7)
         ev_out(7, "s", slice(0, 256))
         store(7, slice(0, 256))
         ev_out(7, "v", slice(256, 512))

@@ -9,218 +9,224 @@ U32 = mybir.dt.uint32
 U8 = mybir.dt.uint8
 E4M3X4 = mybir.dt.float8_e4m3fn_x4
 E5M2X4 = mybir.dt.float8_e5m2_x4
-ACT = mybir.ActivationFunctionType
+EXP = mybir.ActivationFunctionType.Exp
+COPY = mybir.ActivationFunctionType.Copy
 MULT = mybir.AluOpType.mult
 ADD = mybir.AluOpType.add
 
 M, K, N = 1024, 2048, 512
 BETA = 4.0
 P = 128
+PACK = 4
+PASSES = K // (P * PACK)
 TILES = M // P
-PASSES = K // 512
 FLOPS = 2 * 2 * M * K * N
 
-LATE = tuple(range(2))
-HALF = True
+WARM_START = 7
+WARM_BETWEEN = 2
 
 
 def tile_velocity_connectivity_smoothing_s2_kernel(tc, cosines, conn, degree, gain, coords, out):
     nc = tc.nc
-    cos_rows = cosines.rearrange("(p t) k -> p t k", t=TILES)
-    conn_rows = conn.rearrange("(p t) k -> p t k", t=TILES)
-    out_rows = out.rearrange("(p t) c -> p t c", t=TILES)
-    coords_rows = coords.rearrange("(g p j) w -> g p j w", p=P, j=4)
+    cos_rows = cosines.rearrange("(p n) k -> p n k", n=TILES)
+    conn_rows = conn.rearrange("(p n) k -> p n k", n=TILES)
+    out_rows = out.rearrange("(p n) c -> p n c", n=TILES)
+    coords_rows = coords.rearrange("(g p t) c -> g p t c", p=P, t=PACK)
 
     with ExitStack() as ctx:
         keep = ctx.enter_context(tc.tile_pool(name="keep", bufs=1))
-        ins = ctx.enter_context(tc.tile_pool(name="ins", bufs=1))
         work = ctx.enter_context(tc.tile_pool(name="work", bufs=3))
         banks = ctx.enter_context(tc.psum_pool(name="banks", bufs=6))
         sums = ctx.enter_context(tc.psum_pool(name="sums", bufs=2))
         ctx.enter_context(tc.manual_schedule())
 
-        cos_sb, conn_sb, raw_sb = {}, {}, {}
-        e_codes, e_scales = {}, {}
-        p_sb, a_sb, a_grp, c_grp = {}, {}, {}, {}
-        a_codes, a_scales, c_codes, c_scales = {}, {}, {}, {}
-        bank, acc, res, ordered = {}, {}, {}, {}
+        cos_sb, conn_sb, coords_sb = {}, {}, {}
+        coords_in, coords_codes, coords_scales = {}, {}, {}
+        p_sb, conn_ordered = {}, {}
+        a_in, a_codes, a_scales = {}, {}, {}
+        conn_in, conn_codes, conn_scales = {}, {}, {}
+        p_bank, conn_bank, acc, result = {}, {}, {}, {}
 
-        gain_pt = keep.tile([P, PASSES, 4], BF16, name="gain_pt")
-        gain_f = keep.tile([P, PASSES, 4], F32, name="gain_f")
-        deg = keep.tile([P, TILES], BF16, name="deg")
         ident = keep.tile([P, P], F32, name="ident")
-        gain_row = keep.tile([P, K], BF16, name="gain_row", align_bytes=64)
-        zsum = keep.tile([P, TILES], F32, name="zsum")
-        ztot = keep.tile([P, TILES], F32, name="ztot")
-        rz = keep.tile([P, TILES], F32, name="rz")
-        zhalf = keep.tile([P, 2], F32, name="zhalf")
         zeros = keep.tile([P, N], BF16, name="zeros")
-        dummy = keep.tile([P, 1], F32, name="dummy")
+        gain_bf = keep.tile([P, PASSES, PACK], BF16, name="gain_bf")
+        gain_f32 = keep.tile([P, PASSES, PACK], F32, name="gain_f32")
+        deg = keep.tile([P, TILES], BF16, name="deg")
+        p_sum = keep.tile([P, TILES], F32, name="p_sum")
+        p_sum_halves = keep.tile([P, 2], F32, name="p_sum_halves")
+        z = keep.tile([P, TILES], F32, name="z")
+        z_inv = keep.tile([P, TILES], F32, name="z_inv")
+        first = keep.tile([P, 1], F32, name="first")
 
-        def load_cos(i, h=None):
-            if i not in cos_sb:
-                cos_sb[i] = ins.tile([P, K], BF16, name="cos%d" % i)
-            c = slice(0, K) if h is None else slice(K // 2 * h, K // 2 * (h + 1))
-            nc.sync.dma_start(out=cos_sb[i][:, c], in_=cos_rows[:, i, c])
 
-        def load_conn(i, h=None):
-            if i not in conn_sb:
-                conn_sb[i] = ins.tile([P, K], BF16, name="conn%d" % i)
-            c = slice(0, K) if h is None else slice(K // 2 * h, K // 2 * (h + 1))
-            nc.sync.dma_start(out=conn_sb[i][:, c], in_=conn_rows[:, i, c])
+        def load_cos(n, cols=slice(0, K)):
+            if n not in cos_sb:
+                cos_sb[n] = keep.tile([P, K], BF16, name="cos%d" % n)
+            nc.sync.dma_start(out=cos_sb[n][:, cols], in_=cos_rows[:, n, cols])
 
-        def load_small():
-            nc.sync.dma_start(out=gain_pt[:], in_=gain.rearrange("(g p t) -> p g t", p=P, t=4))
-            nc.sync.dma_start(out=deg[:], in_=degree.rearrange("(p t) -> p t", t=TILES))
-
-        def dummies(n):
-            for k in range(n):
-                nc.tensor.matmul(acc["warm"][:], lhsT=zeros[:, 0:P], rhs=zeros[:], start=True, stop=True)
+        def load_conn(n, cols=slice(0, K)):
+            if n not in conn_sb:
+                conn_sb[n] = keep.tile([P, K], BF16, name="conn%d" % n)
+            nc.sync.dma_start(out=conn_sb[n][:, cols], in_=conn_rows[:, n, cols])
 
         def load_coords(g):
-            raw_sb[g] = ins.tile([P, 4, N], BF16, name="raw%d" % g)
-            nc.sync.dma_start(out=raw_sb[g][:], in_=coords_rows[g])
+            coords_sb[g] = keep.tile([P, PACK, N], BF16, name="coords%d" % g)
+            nc.sync.dma_start(out=coords_sb[g][:], in_=coords_rows[g])
 
-        def interleave(g, eng):
-            t = keep.tile([P, N, 4], BF16, name="egrp%d" % g, align_bytes=64)
-            e_codes[g, "in"] = t
-            dst = t[:].rearrange("p (c i) t -> p c t i", i=4)
-            src = raw_sb[g][:].rearrange("p t (c i) -> p c t i", i=4)
-            if eng == "v":
-                nc.vector.tensor_copy(out=dst, in_=src)
-            elif eng == "g":
-                for c in range(2):
-                    w = slice(64 * c, 64 * (c + 1))
-                    nc.gpsimd.tensor_scalar(out=dst[:, w], in0=src[:, w], scalar1=1.0, scalar2=0.0, op0=MULT, op1=ADD)
-            else:
-                nc.scalar.copy(dst, src)
+        def store(n, cols=slice(0, N)):
+            nc.sync.dma_start(out=out_rows[:, n, cols], in_=result[n][:, cols])
 
-        def q_coords(g):
-            e_codes[g] = keep.tile([P, N], U32, name="ecodes%d" % g, align_bytes=64)
-            e_scales[g] = keep.tile([P, N], U8, name="escales%d" % g, align_bytes=64)
-            nc.vector.quantize_mx(out=e_codes[g][:].bitcast(E4M3X4), scales=e_scales[g][:], in_=e_codes[g, "in"][:].rearrange("p w j -> p (w j)"))
+        def warm(count):
+            for repeat in range(count):
+                nc.tensor.matmul(acc["warm"][:], lhsT=zeros[:, 0:P], rhs=zeros[:], start=True, stop=True)
 
-        def load_gain_row(g):
-            c = slice(512 * g, 512 * (g + 1))
-            nc.sync.dma_start(out=gain_row[:, c], in_=gain[c].partition_broadcast(P))
 
-        def exp_half(i, h):
-            if h == 0:
-                p_sb[i] = work.tile([P, K], F32, name="p", align_bytes=64)
-            n = slice(256 * h, 256 * (h + 1))
-            src = cos_sb[i][:].rearrange("p (n t) -> p t n", t=4)[:, :, n]
-            dst = p_sb[i][:].rearrange("p (t n) -> p t n", t=4)[:, :, n]
-            nc.scalar.activation(out=dst, in_=src, func=ACT.Exp, scale=BETA, accum_out=zhalf[:, h:h + 1])
+        def interleave_coords(g, copy):
+            coords_in[g] = keep.tile([P, N, PACK], BF16, name="coords_in%d" % g, align_bytes=64)
+            copy(
+                out=coords_in[g][:].rearrange("p (c i) t -> p c t i", i=4),
+                in_=coords_sb[g][:].rearrange("p t (c i) -> p c t i", i=4),
+            )
 
-        def exp(i):
-            p_sb[i] = work.tile([P, K], F32, name="p", align_bytes=64)
-            if i in LATE:
-                src = cos_sb[i][:].rearrange("p (n t) -> p t n", t=4)
-                dst = p_sb[i][:].rearrange("p (t n) -> p t n", t=4)
-            else:
-                src = cos_sb[i][:].rearrange("p (n u e) -> p u n e", u=2, e=2)
-                dst = p_sb[i][:].rearrange("p (u n e) -> p u n e", u=2, e=2)
-            nc.scalar.activation(out=dst, in_=src, func=ACT.Exp, scale=BETA, accum_out=zsum[:, i:i + 1])
+        def quantise_coords(g):
+            coords_codes[g] = keep.tile([P, N], U32, name="coords_codes%d" % g, align_bytes=64)
+            coords_scales[g] = keep.tile([P, N], U8, name="coords_scales%d" % g, align_bytes=64)
+            nc.vector.quantize_mx(
+                out=coords_codes[g][:].bitcast(E4M3X4), scales=coords_scales[g][:],
+                in_=coords_in[g][:].rearrange("p c t -> p (c t)"),
+            )
 
-        def mul(i, h=None):
-            if not h:
-                a_sb[i] = work.tile([P, 2, K // 4, 2], BF16, name="a", align_bytes=64)
-            n = slice(0, 512) if h is None else slice(256 * h, 256 * (h + 1))
-            nc.vector.tensor_tensor(
-                out=a_sb[i][:, :, n, :],
-                in0=p_sb[i][:].rearrange("p (u n e) -> p u n e", u=2, e=2)[:, :, n, :],
-                in1=gain_row[:].rearrange("p (n u e) -> p u n e", u=2, e=2)[:, :, n, :],
-                op=MULT)
 
-        def reorder(i):
-            ordered[i] = work.tile([P, 2, K // 4], F32, name="ordered", align_bytes=64)
-            nc.vector.tensor_copy(out=ordered[i][:], in_=conn_sb[i][:].bitcast(F32).rearrange("p (n u) -> p u n", u=2))
+        def exponentiate(n, half=None):
+            if not half:
+                p_sb[n] = work.tile([P, K], F32, name="p_sb", align_bytes=64)
+            q = slice(0, K // PACK) if half is None else slice(K // PACK // 2 * half, K // PACK // 2 * (half + 1))
+            nc.scalar.activation(
+                out=p_sb[n][:].rearrange("p (t q) -> p t q", t=PACK)[:, :, q],
+                in_=cos_sb[n][:].rearrange("p (q t) -> p t q", t=PACK)[:, :, q],
+                func=EXP, scale=BETA,
+                accum_out=p_sum[:, n:n + 1] if half is None else p_sum_halves[:, half:half + 1],
+            )
 
-        def tr_conn(i, h):
-            b = banks.tile([P, 2, 2 * P], F32, name="bank")
-            bank["c", i, h] = b
-            words = conn_sb[i][:].bitcast(F32)
-            for g in (2 * h, 2 * h + 1):
-                for u in range(2):
-                    src = ordered[i][:, u, P * g:P * (g + 1)] if i in ordered else words[:, 256 * g + u:256 * (g + 1):2]
-                    nc.tensor.transpose(b[:, u, P * (g % 2):P * (g % 2 + 1)], src, ident[:])
+        def invert_z(n):
+            if n == 0:
+                nc.vector.tensor_tensor(out=p_sum[:, 0:1], in0=p_sum_halves[:, 0:1], in1=p_sum_halves[:, 1:2], op=ADD)
+            pair = slice(n, n + 2)
+            nc.vector.tensor_tensor(out=z[:, pair], in0=p_sum[:, pair], in1=deg[:, pair], op=ADD)
+            nc.vector.reciprocal(out=z_inv[:, pair], in_=z[:, pair])
 
-        def tr_a(i, h):
-            b = banks.tile([P, 2, 2 * P], F32, name="bank")
-            bank["a", i, h] = b
-            for g in (2 * h, 2 * h + 1):
-                for u in range(2):
-                    nc.tensor.transpose(b[:, u, P * (g % 2):P * (g % 2 + 1)], a_sb[i][:, u, P * g:P * (g + 1), :].rearrange("p n e -> p (n e)").bitcast(F32), ident[:])
+        def turn_p(n, passes=range(PASSES)):
+            for g in passes:
+                p_bank[n, g] = banks.tile([P, PACK, P], F32, name="bank")
+                for t in range(PACK):
+                    first_col = K // PACK * t + P * g
+                    nc.tensor.transpose(p_bank[n, g][:, t, :], p_sb[n][:, first_col:first_col + P], ident[:])
 
-        def tr_late(i, g):
-            b = banks.tile([P, 4, P], F32, name="bank")
-            bank["a", i, g] = b
-            for t in range(4):
-                nc.tensor.transpose(b[:, t, :], p_sb[i][:, 512 * t + P * g:512 * t + P * (g + 1)], ident[:])
+        def weigh(n, passes=range(PASSES)):
+            if n not in a_in:
+                a_in[n] = work.tile([P, PASSES, P, PACK], BF16, name="a_in", align_bytes=64)
+            for g in passes:
+                nc.vector.tensor_tensor(
+                    out=a_in[n][:, g, :, :],
+                    in0=p_bank[n, g][:].rearrange("p t i -> p i t"),
+                    in1=gain_f32[:, g, :].unsqueeze(1).to_broadcast([P, P, PACK]),
+                    op=MULT,
+                )
 
-        def ev(kind, i, h, eng):
-            grp = c_grp if kind == "c" else a_grp
-            if i not in grp:
-                grp[i] = work.tile([P, 2, 2 * P, 4], BF16, name=kind + "grp", align_bytes=64)
-            dst = grp[i][:, h, :, :].rearrange("p r t -> p (r t)").bitcast(F32).rearrange("p (r u) -> p r u", u=2)
-            src = bank[kind, i, h][:].rearrange("p u r -> p r u")
-            if eng == "v":
-                nc.vector.tensor_copy(out=dst, in_=src)
-            else:
-                nc.scalar.copy(dst, src)
+        def quantise_a(n, passes=slice(0, PASSES)):
+            if passes.start == 0:
+                a_codes[n] = work.tile([P, PASSES * P], U32, name="a_codes", align_bytes=64)
+                a_scales[n] = work.tile([P, PASSES * P], U8, name="a_scales", align_bytes=64)
+            words = slice(P * passes.start, P * passes.stop)
+            nc.vector.quantize_mx(
+                out=a_codes[n][:, words].bitcast(E5M2X4), scales=a_scales[n][:, words],
+                in_=a_in[n][:].rearrange("p g i t -> p (g i t)")[:, PACK * words.start:PACK * words.stop],
+            )
 
-        def ev_late(i, g):
-            if i not in a_grp:
-                a_grp[i] = work.tile([P, 2, 2 * P, 4], BF16, name="agrp", align_bytes=64)
-            dst = a_grp[i][:, g // 2, P * (g % 2):P * (g % 2 + 1), :]
-            nc.vector.tensor_tensor(out=dst, in0=bank["a", i, g][:].rearrange("p t r -> p r t"), in1=gain_f[:, g, :].unsqueeze(1).to_broadcast([P, P, 4]), op=MULT)
 
-        def quant(kind, i, h=None):
-            grp, codes, scales, dt = (c_grp, c_codes, c_scales, E4M3X4) if kind == "c" else (a_grp, a_codes, a_scales, E5M2X4)
-            if not h:
-                codes[i] = work.tile([P, 512], U32, name=kind + "codes", align_bytes=64)
-                scales[i] = work.tile([P, 512], U8, name=kind + "scales", align_bytes=64)
-            w = slice(0, 512) if h is None else slice(256 * h, 256 * (h + 1))
-            nc.vector.quantize_mx(out=codes[i][:, w].bitcast(dt), scales=scales[i][:, w], in_=grp[i][:].rearrange("p h r t -> p (h r t)")[:, 4 * w.start:4 * w.stop])
+        def order_conn(n):
+            conn_ordered[n] = work.tile([P, 2, K // PACK], F32, name="conn_ordered", align_bytes=64)
+            nc.vector.tensor_copy(out=conn_ordered[n][:], in_=conn_sb[n][:].bitcast(F32).rearrange("p (q u) -> p u q", u=2))
 
-        def mm(kind, i, gs=None):
-            codes, scales, dt = (c_codes, c_scales, E4M3X4) if kind == "c" else (a_codes, a_scales, E5M2X4)
-            for g in range(PASSES) if gs is None else gs:
-                if kind == "c" and g == 0:
-                    acc[i] = sums.tile([P, N], F32, name="acc")
+        def turn_conn(n):
+            for half in range(2):
+                conn_bank[n, half] = banks.tile([P, 2, 2 * P], F32, name="bank")
+                for g in (2 * half, 2 * half + 1):
+                    for u in range(2):
+                        if n in conn_ordered:
+                            words = conn_ordered[n][:, u, P * g:P * (g + 1)]
+                        else:
+                            words = conn_sb[n][:].bitcast(F32)[:, 2 * P * g + u:2 * P * (g + 1):2]
+                        nc.tensor.transpose(conn_bank[n, half][:, u, P * (g % 2):P * (g % 2 + 1)], words, ident[:])
+
+        def empty_conn(n, half, copy):
+            if half == 0:
+                conn_in[n] = work.tile([P, 2, 2 * P * PACK], BF16, name="conn_in", align_bytes=64)
+            copy(
+                out=conn_in[n][:, half, :].bitcast(F32).rearrange("p (i u) -> p i u", u=2),
+                in_=conn_bank[n, half][:].rearrange("p u i -> p i u"),
+            )
+
+        def quantise_conn(n):
+            conn_codes[n] = work.tile([P, PASSES * P], U32, name="conn_codes", align_bytes=64)
+            conn_scales[n] = work.tile([P, PASSES * P], U8, name="conn_scales", align_bytes=64)
+            nc.vector.quantize_mx(
+                out=conn_codes[n][:].bitcast(E4M3X4), scales=conn_scales[n][:],
+                in_=conn_in[n][:].rearrange("p h w -> p (h w)"),
+            )
+
+
+        def multiply_conn(n, passes=range(PASSES)):
+            for g in passes:
+                if g == 0:
+                    acc[n] = sums.tile([P, N], F32, name="acc")
                 cols = slice(P * g, P * (g + 1))
                 nc.tensor.matmul_mx(
-                    out=acc[i][:], lhsT=codes[i][:, cols].bitcast(dt), lhsT_scale=scales[i][:, cols],
-                    rhs=e_codes[g][:].bitcast(E4M3X4), rhs_scale=e_scales[g][:],
-                    start=(kind == "c" and g == 0), stop=(kind == "a" and g == PASSES - 1))
+                    out=acc[n][:], lhsT=conn_codes[n][:, cols].bitcast(E4M3X4), lhsT_scale=conn_scales[n][:, cols],
+                    rhs=coords_codes[g][:].bitcast(E4M3X4), rhs_scale=coords_scales[g][:], start=(g == 0), stop=False,
+                )
 
-        def zrec(lo, hi):
-            if HALF and lo == 0:
-                nc.vector.tensor_tensor(out=zsum[:, 0:1], in0=zhalf[:, 0:1], in1=zhalf[:, 1:2], op=ADD)
-            nc.vector.tensor_tensor(out=ztot[:, lo:hi], in0=zsum[:, lo:hi], in1=deg[:, lo:hi], op=ADD)
-            nc.vector.reciprocal(out=rz[:, lo:hi], in_=ztot[:, lo:hi])
+        def multiply_a(n, passes=range(PASSES)):
+            for g in passes:
+                cols = slice(P * g, P * (g + 1))
+                nc.tensor.matmul_mx(
+                    out=acc[n][:], lhsT=a_codes[n][:, cols].bitcast(E5M2X4), lhsT_scale=a_scales[n][:, cols],
+                    rhs=coords_codes[g][:].bitcast(E4M3X4), rhs_scale=coords_scales[g][:], start=False, stop=(g == PASSES - 1),
+                )
 
-        def ev_out(i, eng, c=slice(0, N)):
-            if c.start == 0:
-                res[i] = work.tile([P, N], F32, name="res")
-            if eng == "v":
-                nc.vector.tensor_scalar(out=res[i][:, c], in0=acc[i][:, c], scalar1=rz[:, i:i + 1], scalar2=None, op0=MULT)
-            else:
-                nc.scalar.activation(out=res[i][:, c], in_=acc[i][:, c], func=ACT.Copy, scale=rz[:, i:i + 1])
+        def multiply_pair(g):
+            for n in (0, 1):
+                multiply_conn(n, (g,))
+                multiply_a(n, (g,))
 
-        def store(i, c=slice(0, N)):
-            nc.sync.dma_start(out=out_rows[:, i, c], in_=res[i][:, c])
+        def divide(n):
+            result[n] = work.tile([P, N], F32, name="result")
+            nc.scalar.activation(out=result[n][:], in_=acc[n][:], func=COPY, scale=z_inv[:, n:n + 1])
+            store(n)
+
+        def divide_last(n):
+            result[n] = work.tile([P, N], F32, name="result")
+            left, right = slice(0, N // 2), slice(N // 2, N)
+            nc.scalar.activation(out=result[n][:, left], in_=acc[n][:, left], func=COPY, scale=z_inv[:, n:n + 1])
+            store(n, left)
+            nc.vector.tensor_scalar(
+                out=result[n][:, right], in0=acc[n][:, right], scalar1=z_inv[:, n:n + 1], scalar2=None, op0=MULT)
+            store(n, right)
+
+        on_vector, on_scalar = nc.vector.tensor_copy, nc.scalar.copy
+        first_half, second_half = slice(0, K // 2), slice(K // 2, K)
 
         nc.vector.memset(zeros[:], 0.0)
-        nc.vector.memset(dummy[:], 0.0)
+        nc.vector.memset(first[:], 0.0)
         make_identity(nc, ident[:])
-        nc.scalar.activation(out=dummy[:], in_=dummy[:], func=ACT.Exp)
-        load_cos(0, 0)
-        load_conn(0, 0)
+        nc.scalar.activation(out=first[:], in_=first[:], func=EXP)
+
+        load_cos(0, first_half)
+        load_conn(0, first_half)
         load_coords(0)
-        load_small()
-        load_cos(0, 1)
-        load_conn(0, 1)
+        nc.sync.dma_start(out=gain_bf[:], in_=gain.rearrange("(g p t) -> p g t", p=P, t=PACK))
+        load_cos(0, second_half)
+        load_conn(0, second_half)
         load_cos(1)
         load_coords(1)
         load_conn(1)
@@ -228,192 +234,87 @@ def tile_velocity_connectivity_smoothing_s2_kernel(tc, cosines, conn, degree, ga
         load_coords(3)
         load_cos(2)
         load_conn(2)
-        load_gain_row(0)
-        load_gain_row(1)
-        load_gain_row(2)
-        load_gain_row(3)
-        load_cos(3)
-        load_conn(3)
-        load_cos(4)
-        load_conn(4)
-        load_cos(5)
-        load_conn(5)
-        load_cos(6)
-        load_conn(6)
-        load_cos(7)
-        load_conn(7)
+        nc.sync.dma_start(out=deg[:], in_=degree.rearrange("(p n) -> p n", n=TILES))
+        for n in range(3, TILES):
+            load_cos(n)
+            load_conn(n)
+
         acc["warm"] = sums.tile([P, N], F32, name="acc")
-        dummies(7)
-        exp_half(0, 0)
-        exp_half(0, 1)
-        interleave(0, "v")
-        nc.vector.tensor_copy(out=gain_f[:], in_=gain_pt[:])
-        tr_late(0, 0)
-        tr_late(0, 1)
-        dummies(2)
-        tr_conn(0, 0)
-        tr_conn(0, 1)
-        dummies(2)
-        tr_late(0, 2)
-        tr_late(0, 3)
-        ev_late(0, 0)
-        ev_late(0, 1)
-        q_coords(0)
-        ev("c", 0, 0, "s")
-        ev("c", 0, 1, "s")
-        exp(1)
-        interleave(1, "v")
-        ev_late(0, 2)
-        ev_late(0, 3)
-        quant("c", 0)
-        dummies(2)
-        tr_conn(1, 0)
-        tr_conn(1, 1)
-        dummies(2)
-        tr_late(1, 0)
-        tr_late(1, 1)
-        tr_late(1, 2)
-        tr_late(1, 3)
-        ev("c", 1, 0, "s")
-        ev("c", 1, 1, "v")
-        quant("a", 0)
-        mm("c", 0, (0,))
-        mm("a", 0, (0,))
-        ev_late(1, 0)
-        ev_late(1, 1)
-        ev_late(1, 2)
-        ev_late(1, 3)
-        tr_conn(2, 0)
-        tr_conn(2, 1)
-        quant("c", 1)
-        quant("a", 1)
-        q_coords(1)
-        interleave(2, "s")
-        mm("c", 1, (0,))
-        mm("a", 1, (0,))
-        mm("c", 0, (1,))
-        mm("a", 0, (1,))
-        mm("c", 1, (1,))
-        mm("a", 1, (1,))
-        exp(2)
-        interleave(3, "s")
-        exp(3)
-        mul(2, 0)
-        mul(2, 1)
-        tr_a(2, 0)
-        tr_a(2, 1)
-        q_coords(2)
-        q_coords(3)
-        mm("c", 0, (2,))
-        mm("a", 0, (2,))
-        mm("c", 1, (2,))
-        mm("a", 1, (2,))
-        mm("c", 0, (3,))
-        mm("a", 0, (3,))
-        mm("c", 1, (3,))
-        mm("a", 1, (3,))
-        ev("c", 2, 0, "s")
-        ev("c", 2, 1, "v")
-        zrec(0, 2)
-        ev("a", 2, 0, "s")
-        ev_out(0, "s")
-        store(0)
-        ev("a", 2, 1, "s")
-        exp(4)
-        quant("c", 2)
-        mul(3, 0)
-        mul(3, 1)
-        quant("a", 2)
-        ev_out(1, "v")
-        store(1)
-        tr_conn(3, 0)
-        tr_conn(3, 1)
-        mm("c", 2, (0, 1, 2, 3,))
-        tr_a(3, 0)
-        tr_a(3, 1)
-        mm("a", 2, (0, 1, 2, 3,))
-        ev("c", 3, 0, "s")
-        ev("c", 3, 1, "v")
-        ev("a", 3, 0, "s")
-        ev("a", 3, 1, "s")
-        zrec(2, 4)
-        exp(5)
-        quant("c", 3)
-        mul(4, 0)
-        mul(4, 1)
-        quant("a", 3)
-        tr_conn(4, 0)
-        tr_conn(4, 1)
-        mm("c", 3, (0, 1, 2, 3,))
-        tr_a(4, 0)
-        tr_a(4, 1)
-        mm("a", 3, (0, 1, 2, 3,))
-        ev("c", 4, 0, "s")
-        ev("c", 4, 1, "v")
-        ev("a", 4, 0, "s")
-        ev_out(2, "s")
-        store(2)
-        ev("a", 4, 1, "s")
-        exp(6)
-        quant("c", 4)
-        mul(5, 0)
-        mul(5, 1)
-        quant("a", 4)
-        tr_conn(5, 0)
-        tr_conn(5, 1)
-        mm("c", 4, (0, 1, 2, 3,))
-        tr_a(5, 0)
-        tr_a(5, 1)
-        mm("a", 4, (0, 1, 2, 3,))
-        ev("c", 5, 0, "s")
-        ev("c", 5, 1, "v")
-        ev("a", 5, 0, "s")
-        ev_out(3, "v")
-        store(3)
-        ev("a", 5, 1, "s")
-        zrec(4, 6)
-        exp(7)
-        quant("c", 5)
-        mul(6, 0)
-        mul(6, 1)
-        quant("a", 5)
-        tr_conn(6, 0)
-        tr_conn(6, 1)
-        mm("c", 5, (0, 1, 2, 3,))
-        tr_a(6, 0)
-        tr_a(6, 1)
-        mm("a", 5, (0, 1, 2, 3,))
-        ev("c", 6, 0, "s")
-        ev("c", 6, 1, "v")
-        ev("a", 6, 0, "s")
-        ev_out(4, "s")
-        store(4)
-        ev("a", 6, 1, "s")
-        quant("c", 6)
-        mul(7, 0)
-        mul(7, 1)
-        quant("a", 6)
-        tr_conn(7, 0)
-        tr_conn(7, 1)
-        mm("c", 6, (0, 1, 2, 3,))
-        tr_a(7, 0)
-        tr_a(7, 1)
-        mm("a", 6, (0, 1, 2, 3,))
-        ev("c", 7, 0, "s")
-        ev("c", 7, 1, "v")
-        ev("a", 7, 0, "s")
-        ev_out(5, "v")
-        store(5)
-        ev("a", 7, 1, "s")
-        zrec(6, 8)
-        quant("c", 7)
-        quant("a", 7, 0)
-        quant("a", 7, 1)
-        mm("c", 7, (0, 1, 2, 3,))
-        mm("a", 7, (0, 1, 2, 3,))
-        ev_out(6, "s")
-        store(6)
-        ev_out(7, "s", slice(0, 256))
-        store(7, slice(0, 256))
-        ev_out(7, "v", slice(256, 512))
-        store(7, slice(256, 512))
+        warm(WARM_START)
+        exponentiate(0, half=0)
+        exponentiate(0, half=1)
+        nc.vector.tensor_copy(out=gain_f32[:], in_=gain_bf[:])
+        turn_p(0, (0, 1))
+        warm(WARM_BETWEEN)
+        turn_conn(0)
+        warm(WARM_BETWEEN)
+        turn_p(0, (2, 3))
+        weigh(0, (0, 1))
+        interleave_coords(0, on_vector)
+        empty_conn(0, 0, on_scalar)
+        empty_conn(0, 1, on_vector)
+        exponentiate(1)
+        weigh(0, (2, 3))
+        quantise_coords(0)
+        quantise_conn(0)
+        quantise_a(0)
+        interleave_coords(1, on_scalar)
+        warm(WARM_BETWEEN)
+        turn_conn(1)
+        warm(WARM_BETWEEN)
+        turn_p(1)
+        empty_conn(1, 0, on_vector)
+        empty_conn(1, 1, on_scalar)
+        weigh(1)
+        multiply_conn(0, (0,))
+        multiply_a(0, (0,))
+        turn_conn(2)
+        quantise_conn(1)
+        quantise_a(1)
+        quantise_coords(1)
+        invert_z(0)
+        exponentiate(2)
+        interleave_coords(3, on_vector)
+        interleave_coords(2, on_scalar)
+        multiply_conn(1, (0,))
+        multiply_a(1, (0,))
+        multiply_pair(1)
+        turn_p(2)
+        quantise_coords(2)
+        quantise_coords(3)
+        multiply_pair(2)
+        multiply_pair(3)
+        empty_conn(2, 0, on_scalar)
+        empty_conn(2, 1, on_scalar)
+        exponentiate(3)
+        divide(0)
+        order_conn(3)
+        quantise_conn(2)
+        weigh(2)
+        quantise_a(2)
+
+        for n in range(3, TILES):
+            last = n == TILES - 1
+            turn_conn(n)
+            multiply_conn(n - 1)
+            turn_p(n)
+            multiply_a(n - 1)
+            empty_conn(n, 0, on_scalar)
+            empty_conn(n, 1, on_scalar)
+            divide(n - 2)
+            if not last:
+                exponentiate(n + 1)
+                order_conn(n + 1)
+            quantise_conn(n)
+            if n % 2 == 1:
+                invert_z(n - 1)
+            weigh(n)
+            if not last:
+                quantise_a(n)
+            else:
+                quantise_a(n, slice(0, 2))
+                quantise_a(n, slice(2, 4))
+        multiply_conn(TILES - 1)
+        multiply_a(TILES - 1)
+        divide(TILES - 2)
+        divide_last(TILES - 1)

from contextlib import ExitStack

import concourse.mybir as mybir
from concourse.masks import make_identity

F32 = mybir.dt.float32
BF16 = mybir.dt.bfloat16
U32 = mybir.dt.uint32
U8 = mybir.dt.uint8
E4M3X4 = mybir.dt.float8_e4m3fn_x4
E5M2X4 = mybir.dt.float8_e5m2_x4
EXP = mybir.ActivationFunctionType.Exp
COPY = mybir.ActivationFunctionType.Copy
MULT = mybir.AluOpType.mult
ADD = mybir.AluOpType.add

M, K, N = 1024, 2048, 512
BETA = 4.0
P = 128
PACK = 4
PASSES = K // (P * PACK)
TILES = M // P
FLOPS = 2 * 2 * M * K * N

WARM_START = 7
WARM_BETWEEN = 2


def tile_velocity_connectivity_smoothing_s2_kernel(tc, cosines, conn, degree, gain, coords, out):
    nc = tc.nc
    cos_rows = cosines.rearrange("(p n) k -> p n k", n=TILES)
    conn_rows = conn.rearrange("(p n) k -> p n k", n=TILES)
    out_rows = out.rearrange("(p n) c -> p n c", n=TILES)
    coords_rows = coords.rearrange("(g p t) c -> g p t c", p=P, t=PACK)

    with ExitStack() as ctx:
        keep = ctx.enter_context(tc.tile_pool(name="keep", bufs=1))
        work = ctx.enter_context(tc.tile_pool(name="work", bufs=3))
        banks = ctx.enter_context(tc.psum_pool(name="banks", bufs=6))
        sums = ctx.enter_context(tc.psum_pool(name="sums", bufs=2))
        ctx.enter_context(tc.manual_schedule())

        cos_sb, conn_sb, coords_sb = {}, {}, {}
        coords_in, coords_codes, coords_scales = {}, {}, {}
        p_sb, conn_ordered = {}, {}
        a_in, a_codes, a_scales = {}, {}, {}
        conn_in, conn_codes, conn_scales = {}, {}, {}
        p_bank, conn_bank, acc, result = {}, {}, {}, {}

        ident = keep.tile([P, P], F32, name="ident")
        zeros = keep.tile([P, N], BF16, name="zeros")
        gain_bf = keep.tile([P, PASSES, PACK], BF16, name="gain_bf")
        gain_f32 = keep.tile([P, PASSES, PACK], F32, name="gain_f32")
        deg = keep.tile([P, TILES], BF16, name="deg")
        p_sum = keep.tile([P, TILES], F32, name="p_sum")
        p_sum_halves = keep.tile([P, 2], F32, name="p_sum_halves")
        z = keep.tile([P, TILES], F32, name="z")
        z_inv = keep.tile([P, TILES], F32, name="z_inv")
        first = keep.tile([P, 1], F32, name="first")


        def load_cos(n, cols=slice(0, K)):
            if n not in cos_sb:
                cos_sb[n] = keep.tile([P, K], BF16, name="cos%d" % n)
            nc.sync.dma_start(out=cos_sb[n][:, cols], in_=cos_rows[:, n, cols])

        def load_conn(n, cols=slice(0, K)):
            if n not in conn_sb:
                conn_sb[n] = keep.tile([P, K], BF16, name="conn%d" % n)
            nc.sync.dma_start(out=conn_sb[n][:, cols], in_=conn_rows[:, n, cols])

        def load_coords(g):
            coords_sb[g] = keep.tile([P, PACK, N], BF16, name="coords%d" % g)
            nc.sync.dma_start(out=coords_sb[g][:], in_=coords_rows[g])

        def store(n, cols=slice(0, N)):
            nc.sync.dma_start(out=out_rows[:, n, cols], in_=result[n][:, cols])

        def warm(count):
            for repeat in range(count):
                nc.tensor.matmul(acc["warm"][:], lhsT=zeros[:, 0:P], rhs=zeros[:], start=True, stop=True)


        def interleave_coords(g, copy):
            coords_in[g] = keep.tile([P, N, PACK], BF16, name="coords_in%d" % g, align_bytes=64)
            copy(
                out=coords_in[g][:].rearrange("p (c i) t -> p c t i", i=4),
                in_=coords_sb[g][:].rearrange("p t (c i) -> p c t i", i=4),
            )

        def quantise_coords(g):
            coords_codes[g] = keep.tile([P, N], U32, name="coords_codes%d" % g, align_bytes=64)
            coords_scales[g] = keep.tile([P, N], U8, name="coords_scales%d" % g, align_bytes=64)
            nc.vector.quantize_mx(
                out=coords_codes[g][:].bitcast(E4M3X4), scales=coords_scales[g][:],
                in_=coords_in[g][:].rearrange("p c t -> p (c t)"),
            )


        def exponentiate(n, half=None):
            if not half:
                p_sb[n] = work.tile([P, K], F32, name="p_sb", align_bytes=64)
            q = slice(0, K // PACK) if half is None else slice(K // PACK // 2 * half, K // PACK // 2 * (half + 1))
            nc.scalar.activation(
                out=p_sb[n][:].rearrange("p (t q) -> p t q", t=PACK)[:, :, q],
                in_=cos_sb[n][:].rearrange("p (q t) -> p t q", t=PACK)[:, :, q],
                func=EXP, scale=BETA,
                accum_out=p_sum[:, n:n + 1] if half is None else p_sum_halves[:, half:half + 1],
            )

        def invert_z(n):
            if n == 0:
                nc.vector.tensor_tensor(out=p_sum[:, 0:1], in0=p_sum_halves[:, 0:1], in1=p_sum_halves[:, 1:2], op=ADD)
            pair = slice(n, n + 2)
            nc.vector.tensor_tensor(out=z[:, pair], in0=p_sum[:, pair], in1=deg[:, pair], op=ADD)
            nc.vector.reciprocal(out=z_inv[:, pair], in_=z[:, pair])

        def turn_p(n, passes=range(PASSES)):
            for g in passes:
                p_bank[n, g] = banks.tile([P, PACK, P], F32, name="bank")
                for t in range(PACK):
                    first_col = K // PACK * t + P * g
                    nc.tensor.transpose(p_bank[n, g][:, t, :], p_sb[n][:, first_col:first_col + P], ident[:])

        def weigh(n, passes=range(PASSES)):
            if n not in a_in:
                a_in[n] = work.tile([P, PASSES, P, PACK], BF16, name="a_in", align_bytes=64)
            for g in passes:
                nc.vector.tensor_tensor(
                    out=a_in[n][:, g, :, :],
                    in0=p_bank[n, g][:].rearrange("p t i -> p i t"),
                    in1=gain_f32[:, g, :].unsqueeze(1).to_broadcast([P, P, PACK]),
                    op=MULT,
                )

        def quantise_a(n, passes=slice(0, PASSES)):
            if passes.start == 0:
                a_codes[n] = work.tile([P, PASSES * P], U32, name="a_codes", align_bytes=64)
                a_scales[n] = work.tile([P, PASSES * P], U8, name="a_scales", align_bytes=64)
            words = slice(P * passes.start, P * passes.stop)
            nc.vector.quantize_mx(
                out=a_codes[n][:, words].bitcast(E5M2X4), scales=a_scales[n][:, words],
                in_=a_in[n][:].rearrange("p g i t -> p (g i t)")[:, PACK * words.start:PACK * words.stop],
            )


        def order_conn(n):
            conn_ordered[n] = work.tile([P, 2, K // PACK], F32, name="conn_ordered", align_bytes=64)
            nc.vector.tensor_copy(out=conn_ordered[n][:], in_=conn_sb[n][:].bitcast(F32).rearrange("p (q u) -> p u q", u=2))

        def turn_conn(n):
            for half in range(2):
                conn_bank[n, half] = banks.tile([P, 2, 2 * P], F32, name="bank")
                for g in (2 * half, 2 * half + 1):
                    for u in range(2):
                        if n in conn_ordered:
                            words = conn_ordered[n][:, u, P * g:P * (g + 1)]
                        else:
                            words = conn_sb[n][:].bitcast(F32)[:, 2 * P * g + u:2 * P * (g + 1):2]
                        nc.tensor.transpose(conn_bank[n, half][:, u, P * (g % 2):P * (g % 2 + 1)], words, ident[:])

        def empty_conn(n, half, copy):
            if half == 0:
                conn_in[n] = work.tile([P, 2, 2 * P * PACK], BF16, name="conn_in", align_bytes=64)
            copy(
                out=conn_in[n][:, half, :].bitcast(F32).rearrange("p (i u) -> p i u", u=2),
                in_=conn_bank[n, half][:].rearrange("p u i -> p i u"),
            )

        def quantise_conn(n):
            conn_codes[n] = work.tile([P, PASSES * P], U32, name="conn_codes", align_bytes=64)
            conn_scales[n] = work.tile([P, PASSES * P], U8, name="conn_scales", align_bytes=64)
            nc.vector.quantize_mx(
                out=conn_codes[n][:].bitcast(E4M3X4), scales=conn_scales[n][:],
                in_=conn_in[n][:].rearrange("p h w -> p (h w)"),
            )


        def multiply_conn(n, passes=range(PASSES)):
            for g in passes:
                if g == 0:
                    acc[n] = sums.tile([P, N], F32, name="acc")
                cols = slice(P * g, P * (g + 1))
                nc.tensor.matmul_mx(
                    out=acc[n][:], lhsT=conn_codes[n][:, cols].bitcast(E4M3X4), lhsT_scale=conn_scales[n][:, cols],
                    rhs=coords_codes[g][:].bitcast(E4M3X4), rhs_scale=coords_scales[g][:], start=(g == 0), stop=False,
                )

        def multiply_a(n, passes=range(PASSES)):
            for g in passes:
                cols = slice(P * g, P * (g + 1))
                nc.tensor.matmul_mx(
                    out=acc[n][:], lhsT=a_codes[n][:, cols].bitcast(E5M2X4), lhsT_scale=a_scales[n][:, cols],
                    rhs=coords_codes[g][:].bitcast(E4M3X4), rhs_scale=coords_scales[g][:], start=False, stop=(g == PASSES - 1),
                )

        def multiply_pair(g):
            for n in (0, 1):
                multiply_conn(n, (g,))
                multiply_a(n, (g,))

        def divide(n):
            result[n] = work.tile([P, N], F32, name="result")
            nc.scalar.activation(out=result[n][:], in_=acc[n][:], func=COPY, scale=z_inv[:, n:n + 1])
            store(n)

        def divide_last(n):
            result[n] = work.tile([P, N], F32, name="result")
            left, right = slice(0, N // 2), slice(N // 2, N)
            nc.scalar.activation(out=result[n][:, left], in_=acc[n][:, left], func=COPY, scale=z_inv[:, n:n + 1])
            store(n, left)
            nc.vector.tensor_scalar(
                out=result[n][:, right], in0=acc[n][:, right], scalar1=z_inv[:, n:n + 1], scalar2=None, op0=MULT)
            store(n, right)

        on_vector, on_scalar = nc.vector.tensor_copy, nc.scalar.copy
        first_half, second_half = slice(0, K // 2), slice(K // 2, K)

        nc.vector.memset(zeros[:], 0.0)
        nc.vector.memset(first[:], 0.0)
        make_identity(nc, ident[:])
        nc.scalar.activation(out=first[:], in_=first[:], func=EXP)

        load_cos(0, first_half)
        load_conn(0, first_half)
        load_coords(0)
        nc.sync.dma_start(out=gain_bf[:], in_=gain.rearrange("(g p t) -> p g t", p=P, t=PACK))
        load_cos(0, second_half)
        load_conn(0, second_half)
        load_cos(1)
        load_coords(1)
        load_conn(1)
        load_coords(2)
        load_coords(3)
        load_cos(2)
        load_conn(2)
        nc.sync.dma_start(out=deg[:], in_=degree.rearrange("(p n) -> p n", n=TILES))
        for n in range(3, TILES):
            load_cos(n)
            load_conn(n)

        acc["warm"] = sums.tile([P, N], F32, name="acc")
        warm(WARM_START)
        exponentiate(0, half=0)
        exponentiate(0, half=1)
        nc.vector.tensor_copy(out=gain_f32[:], in_=gain_bf[:])
        turn_p(0, (0, 1))
        warm(WARM_BETWEEN)
        turn_conn(0)
        warm(WARM_BETWEEN)
        turn_p(0, (2, 3))
        weigh(0, (0, 1))
        interleave_coords(0, on_vector)
        empty_conn(0, 0, on_scalar)
        empty_conn(0, 1, on_vector)
        exponentiate(1)
        weigh(0, (2, 3))
        quantise_coords(0)
        quantise_conn(0)
        quantise_a(0)
        interleave_coords(1, on_scalar)
        warm(WARM_BETWEEN)
        turn_conn(1)
        warm(WARM_BETWEEN)
        turn_p(1)
        empty_conn(1, 0, on_vector)
        empty_conn(1, 1, on_scalar)
        weigh(1)
        multiply_conn(0, (0,))
        multiply_a(0, (0,))
        turn_conn(2)
        quantise_conn(1)
        quantise_a(1)
        quantise_coords(1)
        invert_z(0)
        exponentiate(2)
        interleave_coords(3, on_vector)
        interleave_coords(2, on_scalar)
        multiply_conn(1, (0,))
        multiply_a(1, (0,))
        multiply_pair(1)
        turn_p(2)
        quantise_coords(2)
        quantise_coords(3)
        multiply_pair(2)
        multiply_pair(3)
        empty_conn(2, 0, on_scalar)
        empty_conn(2, 1, on_scalar)
        exponentiate(3)
        divide(0)
        order_conn(3)
        quantise_conn(2)
        weigh(2)
        quantise_a(2)

        for n in range(3, TILES):
            last = n == TILES - 1
            turn_conn(n)
            multiply_conn(n - 1)
            turn_p(n)
            multiply_a(n - 1)
            empty_conn(n, 0, on_scalar)
            empty_conn(n, 1, on_scalar)
            divide(n - 2)
            if not last:
                exponentiate(n + 1)
                order_conn(n + 1)
            quantise_conn(n)
            if n % 2 == 1:
                invert_z(n - 1)
            weigh(n)
            if not last:
                quantise_a(n)
            else:
                quantise_a(n, slice(0, 2))
                quantise_a(n, slice(2, 4))
        multiply_conn(TILES - 1)
        multiply_a(TILES - 1)
        divide(TILES - 2)
        divide_last(TILES - 1)
